import numpy as np
import ml_dtypes


def mxq(x, axis, fmt="e4m3"):
    dtype, down = {"e4m3": (ml_dtypes.float8_e4m3fn, 7), "e5m2": (ml_dtypes.float8_e5m2, 14)}[fmt]
    v = np.moveaxis(np.asarray(x, np.float32).astype(ml_dtypes.bfloat16).astype(np.float64), axis, -1)
    blocks = v.reshape(v.shape[:-1] + (-1, 32))
    amax = np.abs(blocks).max(-1, keepdims=True)
    byte = np.maximum(np.where(amax > 0, np.frexp(amax)[1] - 1 + 127, 0) - down, 1)
    scale = np.exp2(byte - 127.0)
    codes = (blocks / scale).astype(np.float32).astype(dtype).astype(np.float64)
    return np.moveaxis((codes * scale).reshape(v.shape), -1, axis)


WIDE = False


def mx_kscale(k):
    if not WIDE:
        return np.ones(k)
    levels = np.array([10, -10, 5, -5, 0])
    if k % 512:
        return np.exp2(np.random.permutation(np.resize(levels, k // 32))).repeat(32)
    a = np.empty((k // 512, 16))
    for p in range(k // 512):
        a[p, :8] = np.random.permutation(np.resize(levels, 8))
        for g in range(8):
            far = levels[np.abs(levels - a[p, g]) >= 10]
            a[p, g + 8] = far[np.random.randint(len(far))]
    return np.exp2(a.ravel()).repeat(32)


def f64(x):
    return np.asarray(x).astype(np.float64)


def striped(idx):
    return np.tile(idx.reshape(-1, 16).T, (8, 1)).astype(np.uint16)


def unstriped(offs):
    return offs[:16].T.reshape(-1).astype(np.int64)


def pack_weight(w):
    k, n = w.shape
    w = f64(np.asarray(w, np.float32).astype(ml_dtypes.bfloat16)).reshape(k // 32, 32, n)
    amax = np.abs(w).max(1)
    byte = np.clip(np.where(amax > 0, np.frexp(amax)[1] - 1 + 127 - 7, 1), 1, 254)
    scaled = (w * np.exp2(127.0 - byte)[:, None, :]).reshape(k, n).astype(np.float32)
    words = np.ascontiguousarray(scaled.reshape(k // 512, 128, 4, n).transpose(0, 1, 3, 2)).astype(ml_dtypes.float8_e4m3fn).view(np.uint8)
    return words, np.ascontiguousarray(byte.astype(np.uint8).reshape(k // 512, 16, n))


def unpack_weight(words, scales):
    g, p, n, _ = words.shape
    vals = np.ascontiguousarray(words).view(ml_dtypes.float8_e4m3fn).astype(np.float64) * np.repeat(np.exp2(scales.astype(np.float64) - 127.0), 8, axis=1)[..., None]
    return vals.transpose(0, 1, 3, 2).reshape(g * 512, n)


K, T, S, N, D = 1024, 1024, 512, 128, 3
P = 2 ** 7


def setup_inputs():
    n = np.random.standard_normal
    s = mx_kscale(K)[:, None]
    packed_xT = pack_weight(n((K, T)) * s)
    return {
        "x_words": packed_xT[0],
        "x_scales": packed_xT[1],
        "w1": (n((K, N)) / np.sqrt(K) / s).astype(np.float32),
        "sus": (np.random.uniform(0.3, 0.95, (N, S))).astype(np.float32),
        "inf": (np.random.uniform(0.0, 0.3, (N, S)) ** 1.5).astype(np.float32),
        "lat": (np.random.uniform(0.0, 0.2, (N, S))).astype(np.float32),
        "mob": (np.tile(np.random.uniform(0.05, 0.3, (D, 1, S)), (1, P, 1))).astype(np.float32),
        "rate": (np.random.uniform(0.1, 0.6, (N, 1))).astype(np.float32),
        "offs": striped(np.random.permutation(T)[:S]),
        "pos1": striped(np.random.permutation(S)[:S]),
        "pos2": striped(np.random.permutation(S)[:S]),
        "pos3": striped(np.random.permutation(S)[:S]),
    }


def reference(x_words, x_scales, w1, sus, inf, lat, mob, rate, offs, pos1, pos2, pos3):
    xq = unpack_weight(x_words, x_scales)[:, unstriped(offs)]
    y = mxq(f64(w1), 0, "e4m3").T @ xq
    beta = 0.6 * (np.log(np.exp(y) + 1.0))
    bi = beta * f64(inf)
    force = bi + beta * (bi[:, unstriped(pos1)] * f64(mob)[0, :1] + bi[:, unstriped(pos2)] * f64(mob)[1, :1] + bi[:, unstriped(pos3)] * f64(mob)[2, :1])
    newi = f64(sus) * (-1.0 * np.exp(-1.0 * force) + 1.0)
    return f64(lat) + newi - (f64(rate) * f64(lat))

@@ -1,0 +1,206 @@
+import math
+from contextlib import ExitStack
+
+import concourse.mybir as mybir
+from concourse.masks import make_identity
+
+K, T, S, M, D = 1024, 1024, 512, 128, 3
+FLOPS = 2 * K * M * S
+
+F32 = mybir.dt.float32
+BF16 = mybir.dt.bfloat16
+I32 = mybir.dt.int32
+U32 = mybir.dt.uint32
+U16 = mybir.dt.uint16
+U8 = mybir.dt.uint8
+FP8X4 = mybir.dt.float8_e4m3fn_x4
+ALU = mybir.AluOpType
+ACT = mybir.ActivationFunctionType
+
+P = 128
+PACK = 4
+PASSES = K // (P * PACK)
+BLOCKS = S // P
+TURNED = BLOCKS - 1
+HALVES = [(0, 256), (256, 512)]
+KNEE = 32.0
+RATE = 0.6
+SPANS = [(0, 256), (256, 384), (384, 512)]
+
+
+def entries(lst, lo, hi):
+    return lst[:, lo // 16 : hi // 16]
+
+
+def tile_picked_yseir_lat_p_kernel(
+    tc, x_words, x_scales, w1, sus, inf, lat, mob, rate, offs, pos1, pos2, pos3, out
+):
+    nc = tc.nc
+    with ExitStack() as ctx:
+        sb = ctx.enter_context(tc.tile_pool(name="sb", bufs=1))
+        ps = ctx.enter_context(tc.psum_pool(name="ps", bufs=1))
+        banks = [ps.tile([P, S], F32, name=f"bank{b}") for b in range(8)]
+
+        scale_table = sb.tile([P, T], U8, align_bytes=64)
+        nc.vector.memset(scale_table[:].bitcast(I32), 0)
+        warm = sb.tile([P, 1], F32)
+        nc.vector.memset(warm[:], 0.0)
+        for q in range(4):
+            nc.scalar.dma_start(
+                scale_table[32 * q : 32 * q + 4 * PASSES, :].bitcast(I32),
+                x_scales[:, 4 * q : 4 * q + 4, :].bitcast(I32),
+            )
+        warm_out = sb.tile([P, 1], F32)
+        nc.scalar.activation(warm_out[:], warm[:], ACT.Exp)
+
+        offs_sb = sb.tile([P, S // 16], U16)
+        nc.sync.dma_start(offs_sb[:], offs)
+        word_table = [sb.tile([P, T], I32, name=f"word_table{g}", align_bytes=64) for g in range(PASSES)]
+        w_raw = [sb.tile([P, PACK, M], F32, name=f"w_raw{g}") for g in range(PASSES)]
+        w_rows = w1.rearrange("(g p j) m -> g p j m", g=PASSES, j=PACK)
+
+        def load_words(g):
+            nc.sync.dma_start(word_table[g][:], x_words[g].rearrange("p c r -> p (c r)").bitcast(I32))
+
+        load_words(0)
+        for g in range(PASSES):
+            nc.sync.dma_start(w_raw[g][:], w_rows[g])
+        load_words(1)
+        inf_sb = sb.tile([P, S], F32)
+        nc.sync.dma_start(inf_sb[:], inf)
+        mob_rows = sb.tile([P, P], F32)
+        nc.gpsimd.memset(mob_rows[:], 0.0)
+        nc.sync.dma_start(
+            mob_rows[0 : D * BLOCKS, :], mob[:, 0, :].rearrange("d (c j) -> d c j", j=P)
+        )
+        sus_sb = sb.tile([P, S], F32)
+        nc.sync.dma_start(sus_sb[:], sus)
+        lat_sb = sb.tile([P, S], F32)
+        nc.sync.dma_start(lat_sb[:], lat)
+        rate_sb = sb.tile([P, 1], F32)
+        nc.sync.dma_start(rate_sb[:], rate)
+        pos_sb = []
+        for d, pos in enumerate((pos1, pos2, pos3)):
+            lst = sb.tile([P, S // 16], U16, name=f"pos_sb{d}")
+            nc.sync.dma_start(lst[:], pos)
+            pos_sb.append(lst)
+        mob_last = sb.tile([P, D, P], F32)
+        nc.sync.dma_start(mob_last[:], mob[:, :, TURNED * P :].rearrange("d p j -> p d j"))
+        ident = sb.tile([P, P], F32)
+        make_identity(nc, ident[:])
+
+        w_bf = [sb.tile([P, M, PACK], BF16, name=f"w_bf{g}", align_bytes=64) for g in range(PASSES)]
+        w_codes = [sb.tile([P, M], U32, name=f"w_codes{g}", align_bytes=64) for g in range(PASSES)]
+        w_scales = [sb.tile([P, M], U8, name=f"w_scales{g}", align_bytes=64) for g in range(PASSES)]
+        x_codes = [sb.tile([P, S], U32, name=f"x_codes{g}", align_bytes=64) for g in range(PASSES)]
+        x_sc = sb.tile([P, S], U8, align_bytes=64)
+
+        def product(g, n):
+            lo, hi = SPANS[n]
+            nc.tensor.matmul_mx(
+                out=banks[n][:, 0 : hi - lo],
+                lhsT=w_codes[g][:].bitcast(FP8X4),
+                lhsT_scale=w_scales[g][:],
+                rhs=x_codes[g][:, lo:hi].bitcast(FP8X4),
+                rhs_scale=x_sc[4 * g :, lo:hi],
+                start=(g == 0),
+                stop=(g == PASSES - 1),
+            )
+
+        nc.vector.tensor_copy(x_sc[:], scale_table[:].indirect(offs_sb[:]))
+        nc.vector.tensor_copy(x_codes[0][:], word_table[0][:].bitcast(U32).indirect(offs_sb[:]))
+        for g in range(PASSES):
+            nc.scalar.copy(
+                w_bf[g][:].rearrange("p (c i) j -> p c j i", i=4),
+                w_raw[g][:].rearrange("p j (c i) -> p c j i", i=4),
+            )
+            nc.vector.quantize_mx(
+                out=w_codes[g][:].bitcast(FP8X4), scales=w_scales[g][:], in_=w_bf[g][:].rearrange("p m j -> p (m j)")
+            )
+        for n in range(len(SPANS)):
+            product(0, n)
+        growth = sb.tile([P, S], F32)
+        for n, (lo, hi) in enumerate(SPANS):
+            nc.vector.tensor_copy(
+                x_codes[1][:, lo:hi], word_table[1][:].bitcast(U32).indirect(entries(offs_sb, lo, hi))
+            )
+            product(1, n)
+            nc.scalar.activation(growth[:, lo:hi], banks[n][:, 0 : hi - lo], ACT.Exp)
+
+        stretch = sb.tile([P, S], F32)
+        for n, (lo, hi) in enumerate(SPANS):
+            nc.vector.tensor_scalar(stretch[:, lo:hi], banks[n][:, 0 : hi - lo], KNEE, RATE / KNEE, ALU.max, ALU.mult)
+        capped = sb.tile([P, S], F32)
+        nc.vector.tensor_scalar(capped[:], growth[:], math.exp(KNEE), None, ALU.min)
+        stretched_inf = sb.tile([P, S], F32)
+        nc.vector.tensor_tensor(stretched_inf[:], stretch[:], inf_sb[:], ALU.mult)
+        for c in range(TURNED):
+            nc.tensor.transpose(banks[7][:, c * P : (c + 1) * P], inf_sb[:, c * P : (c + 1) * P], ident[:])
+        nc.tensor.transpose(banks[7][:, TURNED * P : (TURNED + 1) * P], mob_rows[:], ident[:])
+        inf_t = sb.tile([P, TURNED * P + D * BLOCKS], F32)
+        nc.vector.tensor_copy(inf_t[:], banks[7][:, 0 : TURNED * P + D * BLOCKS])
+        stay = sb.tile([P, 1], F32)
+        nc.vector.tensor_scalar(stay[:], rate_sb[:], -1.0, 1.0, ALU.mult, ALU.add)
+        base = sb.tile([P, S], F32)
+        nc.vector.scalar_tensor_tensor(base[:], lat_sb[:], stay[:], sus_sb[:], ALU.mult, ALU.add)
+        totals = [banks[3 + c][:, 0:P] for c in range(TURNED)]
+        for c in range(TURNED):
+            nc.tensor.matmul(
+                totals[c], lhsT=inf_t[:, c * P : (c + 1) * P], rhs=ident[:], is_transpose=True, start=True, stop=False
+            )
+
+        logs = sb.tile([P, S], F32)
+        bi = sb.tile([P, S], F32)
+        for lo, hi in HALVES:
+            nc.scalar.activation(logs[:, lo:hi], capped[:, lo:hi], ACT.Ln, bias=1.0)
+            nc.vector.tensor_tensor(bi[:, lo:hi], logs[:, lo:hi], stretched_inf[:, lo:hi], ALU.mult)
+        warm2 = sb.tile([P, 1], F32)
+        nc.scalar.activation(warm2[:], logs[:, S - 1 : S], ACT.Exp)
+
+        escape = sb.tile([P, S], F32)
+        wide = TURNED * P
+        for d in range(D):
+            if d == D - 1:
+                picked = escape[:, S - wide :]
+            else:
+                picked = sb.tile([P, wide], F32, name=f"picked{d}")[:]
+            nc.vector.tensor_copy(picked, bi[:].indirect(entries(pos_sb[d], 0, wide)))
+            turned = []
+            for c in range(TURNED):
+                spot = banks[c][:, 0:P] if d == D - 1 else banks[6 + d][:, c * P : (c + 1) * P]
+                nc.tensor.transpose(spot, picked[:, c * P : (c + 1) * P], ident[:])
+                turned.append(spot)
+            for c in range(TURNED):
+                weighted = sb.tile([P, P], F32, name=f"weighted{c}_{d}")
+                col = wide + BLOCKS * d + c
+                nc.scalar.activation(weighted[:], turned[c], ACT.Copy, scale=inf_t[:, col : col + 1])
+                nc.tensor.matmul(
+                    totals[c], lhsT=weighted[:], rhs=ident[:], is_transpose=True, start=False, stop=(d == D - 1)
+                )
+        running = inf_sb[:, wide:]
+        for d in range(D):
+            weighted = sb.tile([P, P], F32, name=f"weighted_last{d}")
+            nc.vector.tensor_tensor(
+                weighted[:], bi[:].indirect(entries(pos_sb[d], wide, S)), mob_last[:, d, :], ALU.mult
+            )
+            summed = sb.tile([P, P], F32, name=f"summed{d}")
+            nc.vector.tensor_tensor(summed[:], running, weighted[:], ALU.add)
+            running = summed[:]
+        totals.append(running)
+
+        beta = sb.tile([P, S], F32)
+        force = sb.tile([P, S], F32)
+        spared = sb.tile([P, S], F32)
+        result = sb.tile([P, S], F32)
+        for lo, hi in HALVES:
+            nc.vector.tensor_tensor(beta[:, lo:hi], logs[:, lo:hi], stretch[:, lo:hi], ALU.mult)
+        for c in range(BLOCKS):
+            cols = slice(c * P, (c + 1) * P)
+            nc.vector.tensor_tensor(force[:, cols], totals[c], beta[:, cols], ALU.mult)
+        for lo, hi in HALVES:
+            nc.scalar.activation(escape[:, lo:hi], force[:, lo:hi], ACT.Exp, scale=-1.0)
+        for lo, hi in HALVES:
+            nc.vector.tensor_tensor(spared[:, lo:hi], escape[:, lo:hi], sus_sb[:, lo:hi], ALU.mult)
+        for lo, hi in HALVES:
+            nc.vector.tensor_tensor(result[:, lo:hi], base[:, lo:hi], spared[:, lo:hi], ALU.subtract)
+            nc.sync.dma_start(out[:, lo:hi], result[:, lo:hi])

@@ -2,7 +2,6 @@ import math
 from contextlib import ExitStack
 
 import concourse.mybir as mybir
-from concourse.masks import make_identity
 
 K, T, S, M, D = 1024, 1024, 512, 128, 3
 FLOPS = 2 * K * M * S
@@ -39,7 +38,7 @@ def tile_picked_yseir_lat_p_kernel(
     with ExitStack() as ctx:
         sb = ctx.enter_context(tc.tile_pool(name="sb", bufs=1))
         ps = ctx.enter_context(tc.psum_pool(name="ps", bufs=1))
-        banks = [ps.tile([P, S], F32, name=f"bank{b}") for b in range(8)]
+        banks = [ps.tile([P, S], F32, name=f"bank{b}") for b in range(len(SPANS))]
 
         scale_table = sb.tile([P, T], U8, align_bytes=64)
         nc.vector.memset(scale_table[:].bitcast(I32), 0)
@@ -68,11 +67,8 @@ def tile_picked_yseir_lat_p_kernel(
         load_words(1)
         inf_sb = sb.tile([P, S], F32)
         nc.sync.dma_start(inf_sb[:], inf)
-        mob_rows = sb.tile([P, P], F32)
-        nc.gpsimd.memset(mob_rows[:], 0.0)
-        nc.sync.dma_start(
-            mob_rows[0 : D * BLOCKS, :], mob[:, 0, :].rearrange("d (c j) -> d c j", j=P)
-        )
+        mob_sb = sb.tile([P, D, S], F32)
+        nc.sync.dma_start(mob_sb[:], mob.rearrange("d p j -> p d j"))
         sus_sb = sb.tile([P, S], F32)
         nc.sync.dma_start(sus_sb[:], sus)
         lat_sb = sb.tile([P, S], F32)
@@ -84,14 +80,10 @@ def tile_picked_yseir_lat_p_kernel(
             lst = sb.tile([P, S // 16], U16, name=f"pos_sb{d}")
             nc.sync.dma_start(lst[:], pos)
             pos_sb.append(lst)
-        mob_last = sb.tile([P, D, P], F32)
-        nc.sync.dma_start(mob_last[:], mob[:, :, TURNED * P :].rearrange("d p j -> p d j"))
-        ident = sb.tile([P, P], F32)
-        make_identity(nc, ident[:])
 
-        w_bf = [sb.tile([P, M, PACK], BF16, name=f"w_bf{g}", align_bytes=64) for g in range(PASSES)]
-        w_codes = [sb.tile([P, M], U32, name=f"w_codes{g}", align_bytes=64) for g in range(PASSES)]
-        w_scales = [sb.tile([P, M], U8, name=f"w_scales{g}", align_bytes=64) for g in range(PASSES)]
+        w_bf = sb.tile([P, PASSES * M * PACK], BF16, align_bytes=64)
+        w_codes = sb.tile([P, PASSES * M], U32, align_bytes=64)
+        w_scales = sb.tile([P, PASSES * M], U8, align_bytes=64)
         x_codes = [sb.tile([P, S], U32, name=f"x_codes{g}", align_bytes=64) for g in range(PASSES)]
         x_sc = sb.tile([P, S], U8, align_bytes=64)
 
@@ -99,8 +91,8 @@ def tile_picked_yseir_lat_p_kernel(
             lo, hi = SPANS[n]
             nc.tensor.matmul_mx(
                 out=banks[n][:, 0 : hi - lo],
-                lhsT=w_codes[g][:].bitcast(FP8X4),
-                lhsT_scale=w_scales[g][:],
+                lhsT=w_codes[:, g * M : (g + 1) * M].bitcast(FP8X4),
+                lhsT_scale=w_scales[:, g * M : (g + 1) * M],
                 rhs=x_codes[g][:, lo:hi].bitcast(FP8X4),
                 rhs_scale=x_sc[4 * g :, lo:hi],
                 start=(g == 0),
@@ -111,12 +103,10 @@ def tile_picked_yseir_lat_p_kernel(
         nc.vector.tensor_copy(x_codes[0][:], word_table[0][:].bitcast(U32).indirect(offs_sb[:]))
         for g in range(PASSES):
             nc.scalar.copy(
-                w_bf[g][:].rearrange("p (c i) j -> p c j i", i=4),
+                w_bf[:, g * M * PACK : (g + 1) * M * PACK].rearrange("p (c i j) -> p c j i", i=4, j=PACK),
                 w_raw[g][:].rearrange("p j (c i) -> p c j i", i=4),
             )
-            nc.vector.quantize_mx(
-                out=w_codes[g][:].bitcast(FP8X4), scales=w_scales[g][:], in_=w_bf[g][:].rearrange("p m j -> p (m j)")
-            )
+        nc.vector.quantize_mx(out=w_codes[:].bitcast(FP8X4), scales=w_scales[:], in_=w_bf[:])
         for n in range(len(SPANS)):
             product(0, n)
         growth = sb.tile([P, S], F32)
@@ -134,20 +124,13 @@ def tile_picked_yseir_lat_p_kernel(
         nc.vector.tensor_scalar(capped[:], growth[:], math.exp(KNEE), None, ALU.min)
         stretched_inf = sb.tile([P, S], F32)
         nc.vector.tensor_tensor(stretched_inf[:], stretch[:], inf_sb[:], ALU.mult)
-        for c in range(TURNED):
-            nc.tensor.transpose(banks[7][:, c * P : (c + 1) * P], inf_sb[:, c * P : (c + 1) * P], ident[:])
-        nc.tensor.transpose(banks[7][:, TURNED * P : (TURNED + 1) * P], mob_rows[:], ident[:])
-        inf_t = sb.tile([P, TURNED * P + D * BLOCKS], F32)
-        nc.vector.tensor_copy(inf_t[:], banks[7][:, 0 : TURNED * P + D * BLOCKS])
+        stretched_mob = [sb.tile([P, S], F32, name=f"stretched_mob{d}") for d in range(D)]
+        for d in range(D):
+            nc.vector.tensor_tensor(stretched_mob[d][:], stretch[:], mob_sb[:, d, :], ALU.mult)
         stay = sb.tile([P, 1], F32)
         nc.vector.tensor_scalar(stay[:], rate_sb[:], -1.0, 1.0, ALU.mult, ALU.add)
         base = sb.tile([P, S], F32)
         nc.vector.scalar_tensor_tensor(base[:], lat_sb[:], stay[:], sus_sb[:], ALU.mult, ALU.add)
-        totals = [banks[3 + c][:, 0:P] for c in range(TURNED)]
-        for c in range(TURNED):
-            nc.tensor.matmul(
-                totals[c], lhsT=inf_t[:, c * P : (c + 1) * P], rhs=ident[:], is_transpose=True, start=True, stop=False
-            )
 
         logs = sb.tile([P, S], F32)
         bi = sb.tile([P, S], F32)
@@ -157,50 +140,27 @@ def tile_picked_yseir_lat_p_kernel(
         warm2 = sb.tile([P, 1], F32)
         nc.scalar.activation(warm2[:], logs[:, S - 1 : S], ACT.Exp)
 
-        escape = sb.tile([P, S], F32)
-        wide = TURNED * P
-        for d in range(D):
-            if d == D - 1:
-                picked = escape[:, S - wide :]
-            else:
-                picked = sb.tile([P, wide], F32, name=f"picked{d}")[:]
-            nc.vector.tensor_copy(picked, bi[:].indirect(entries(pos_sb[d], 0, wide)))
-            turned = []
-            for c in range(TURNED):
-                spot = banks[c][:, 0:P] if d == D - 1 else banks[6 + d][:, c * P : (c + 1) * P]
-                nc.tensor.transpose(spot, picked[:, c * P : (c + 1) * P], ident[:])
-                turned.append(spot)
-            for c in range(TURNED):
-                weighted = sb.tile([P, P], F32, name=f"weighted{c}_{d}")
-                col = wide + BLOCKS * d + c
-                nc.scalar.activation(weighted[:], turned[c], ACT.Copy, scale=inf_t[:, col : col + 1])
-                nc.tensor.matmul(
-                    totals[c], lhsT=weighted[:], rhs=ident[:], is_transpose=True, start=False, stop=(d == D - 1)
-                )
-        running = inf_sb[:, wide:]
-        for d in range(D):
-            weighted = sb.tile([P, P], F32, name=f"weighted_last{d}")
-            nc.vector.tensor_tensor(
-                weighted[:], bi[:].indirect(entries(pos_sb[d], wide, S)), mob_last[:, d, :], ALU.mult
-            )
-            summed = sb.tile([P, P], F32, name=f"summed{d}")
-            nc.vector.tensor_tensor(summed[:], running, weighted[:], ALU.add)
-            running = summed[:]
-        totals.append(running)
-
-        beta = sb.tile([P, S], F32)
+        terms = [sb.tile([P, S], F32, name=f"term{d}") for d in range(D)]
+        sums = [sb.tile([P, S], F32, name=f"sum{d}") for d in range(D)]
         force = sb.tile([P, S], F32)
+        escape = sb.tile([P, S], F32)
         spared = sb.tile([P, S], F32)
         result = sb.tile([P, S], F32)
         for lo, hi in HALVES:
-            nc.vector.tensor_tensor(beta[:, lo:hi], logs[:, lo:hi], stretch[:, lo:hi], ALU.mult)
-        for c in range(BLOCKS):
-            cols = slice(c * P, (c + 1) * P)
-            nc.vector.tensor_tensor(force[:, cols], totals[c], beta[:, cols], ALU.mult)
+            for d in range(D):
+                nc.vector.tensor_tensor(
+                    terms[d][:, lo:hi],
+                    bi[:].indirect(entries(pos_sb[d], lo, hi)),
+                    stretched_mob[d][:, lo:hi],
+                    ALU.mult,
+                )
         for lo, hi in HALVES:
+            for d in range(D):
+                before = stretched_inf if d == 0 else sums[d - 1]
+                nc.vector.tensor_tensor(sums[d][:, lo:hi], before[:, lo:hi], terms[d][:, lo:hi], ALU.add)
+            nc.vector.tensor_tensor(force[:, lo:hi], sums[D - 1][:, lo:hi], logs[:, lo:hi], ALU.mult)
             nc.scalar.activation(escape[:, lo:hi], force[:, lo:hi], ACT.Exp, scale=-1.0)
         for lo, hi in HALVES:
             nc.vector.tensor_tensor(spared[:, lo:hi], escape[:, lo:hi], sus_sb[:, lo:hi], ALU.mult)
-        for lo, hi in HALVES:
             nc.vector.tensor_tensor(result[:, lo:hi], base[:, lo:hi], spared[:, lo:hi], ALU.subtract)
             nc.sync.dma_start(out[:, lo:hi], result[:, lo:hi])

@@ -2,6 +2,7 @@ import math
 from contextlib import ExitStack
 
 import concourse.mybir as mybir
+from concourse.masks import make_identity
 
 K, T, S, M, D = 1024, 1024, 512, 128, 3
 FLOPS = 2 * K * M * S
@@ -38,7 +39,7 @@ def tile_picked_yseir_lat_p_kernel(
     with ExitStack() as ctx:
         sb = ctx.enter_context(tc.tile_pool(name="sb", bufs=1))
         ps = ctx.enter_context(tc.psum_pool(name="ps", bufs=1))
-        banks = [ps.tile([P, S], F32, name=f"bank{b}") for b in range(len(SPANS))]
+        banks = [ps.tile([P, S], F32, name=f"bank{b}") for b in range(8)]
 
         scale_table = sb.tile([P, T], U8, align_bytes=64)
         nc.vector.memset(scale_table[:].bitcast(I32), 0)
@@ -81,6 +82,9 @@ def tile_picked_yseir_lat_p_kernel(
             nc.sync.dma_start(lst[:], pos)
             pos_sb.append(lst)
 
+        ident = sb.tile([P, P], F32)
+        make_identity(nc, ident[:])
+
         w_bf = sb.tile([P, PASSES * M * PACK], BF16, align_bytes=64)
         w_codes = sb.tile([P, PASSES * M], U32, align_bytes=64)
         w_scales = sb.tile([P, PASSES * M], U8, align_bytes=64)
@@ -99,8 +103,8 @@ def tile_picked_yseir_lat_p_kernel(
                 stop=(g == PASSES - 1),
             )
 
-        nc.vector.tensor_copy(x_sc[:], scale_table[:].indirect(offs_sb[:]))
         nc.vector.tensor_copy(x_codes[0][:], word_table[0][:].bitcast(U32).indirect(offs_sb[:]))
+        nc.vector.tensor_copy(x_sc[:], scale_table[:].indirect(offs_sb[:]))
         for g in range(PASSES):
             nc.scalar.copy(
                 w_bf[:, g * M * PACK : (g + 1) * M * PACK].rearrange("p (c i j) -> p c j i", i=4, j=PACK),
@@ -117,50 +121,83 @@ def tile_picked_yseir_lat_p_kernel(
             product(1, n)
             nc.scalar.activation(growth[:, lo:hi], banks[n][:, 0 : hi - lo], ACT.Exp)
 
-        stretch = sb.tile([P, S], F32)
-        for n, (lo, hi) in enumerate(SPANS):
-            nc.vector.tensor_scalar(stretch[:, lo:hi], banks[n][:, 0 : hi - lo], KNEE, RATE / KNEE, ALU.max, ALU.mult)
         capped = sb.tile([P, S], F32)
         nc.vector.tensor_scalar(capped[:], growth[:], math.exp(KNEE), None, ALU.min)
-        stretched_inf = sb.tile([P, S], F32)
-        nc.vector.tensor_tensor(stretched_inf[:], stretch[:], inf_sb[:], ALU.mult)
-        stretched_mob = [sb.tile([P, S], F32, name=f"stretched_mob{d}") for d in range(D)]
-        for d in range(D):
-            nc.vector.tensor_tensor(stretched_mob[d][:], stretch[:], mob_sb[:, d, :], ALU.mult)
+        own = sb.tile([P, S], F32)
+        for n, (lo, hi) in enumerate(SPANS):
+            nc.vector.scalar_tensor_tensor(
+                own[:, lo:hi], banks[n][:, 0 : hi - lo], KNEE, inf_sb[:, lo:hi], ALU.max, ALU.mult
+            )
+        share = sb.tile([P, D, S], F32)
+        for n, (lo, hi) in enumerate(SPANS):
+            nc.vector.scalar_tensor_tensor(
+                share[:, :, lo:hi],
+                banks[n][:, 0 : hi - lo].unsqueeze(1).to_broadcast([P, D, hi - lo]),
+                KNEE,
+                mob_sb[:, :, lo:hi],
+                ALU.max,
+                ALU.mult,
+            )
         stay = sb.tile([P, 1], F32)
         nc.vector.tensor_scalar(stay[:], rate_sb[:], -1.0, 1.0, ALU.mult, ALU.add)
-        base = sb.tile([P, S], F32)
-        nc.vector.scalar_tensor_tensor(base[:], lat_sb[:], stay[:], sus_sb[:], ALU.mult, ALU.add)
+
+        def block(c):
+            return slice(c * P, (c + 1) * P)
+
+        turned = {c: banks[2 + c][:, 0:P] for c in range(1, BLOCKS)}
+        for c in range(1, BLOCKS):
+            nc.tensor.matmul(turned[c], lhsT=own[:, block(c)], rhs=ident[:], is_transpose=True, start=True, stop=False)
 
         logs = sb.tile([P, S], F32)
         bi = sb.tile([P, S], F32)
         for lo, hi in HALVES:
             nc.scalar.activation(logs[:, lo:hi], capped[:, lo:hi], ACT.Ln, bias=1.0)
-            nc.vector.tensor_tensor(bi[:, lo:hi], logs[:, lo:hi], stretched_inf[:, lo:hi], ALU.mult)
+            nc.vector.scalar_tensor_tensor(bi[:, lo:hi], logs[:, lo:hi], RATE / KNEE, own[:, lo:hi], ALU.mult, ALU.mult)
         warm2 = sb.tile([P, 1], F32)
         nc.scalar.activation(warm2[:], logs[:, S - 1 : S], ACT.Exp)
 
-        terms = [sb.tile([P, S], F32, name=f"term{d}") for d in range(D)]
-        sums = [sb.tile([P, S], F32, name=f"sum{d}") for d in range(D)]
-        force = sb.tile([P, S], F32)
         escape = sb.tile([P, S], F32)
-        spared = sb.tile([P, S], F32)
+
+        def neighbour_term(dst, c, d):
+            nc.vector.tensor_tensor(
+                dst, bi[:].indirect(entries(pos_sb[d], c * P, (c + 1) * P)), share[:, d, block(c)], ALU.mult
+            )
+
+        totals = {}
+        for c in range(1, BLOCKS):
+            for d in range(D):
+                if c == BLOCKS - 1 and d == D - 1:
+                    term = escape[:, S // 2 - P // 2 : S // 2 + P // 2]
+                else:
+                    term = sb.tile([P, P], F32, name=f"term{c}_{d}")[:]
+                neighbour_term(term, c, d)
+                nc.tensor.matmul(turned[c], lhsT=term, rhs=ident[:], is_transpose=True, start=False, stop=(d == D - 1))
+            turned_sb = sb.tile([P, P], F32, name=f"turned_sb{c}")
+            nc.scalar.copy(turned_sb[:], turned[c])
+            totals[c] = banks[(5 + c) % 8][:, 0:P]
+            nc.tensor.transpose(totals[c], turned_sb[:], ident[:])
+        running = own[:, block(0)]
+        for d in range(D):
+            term = sb.tile([P, P], F32, name=f"term0_{d}")
+            neighbour_term(term[:], 0, d)
+            summed = sb.tile([P, P], F32, name=f"summed{d}")
+            nc.vector.tensor_tensor(summed[:], running, term[:], ALU.add)
+            running = summed[:]
+        totals[0] = running
+
+        force = sb.tile([P, S], F32)
+        lost = sb.tile([P, S], F32)
         result = sb.tile([P, S], F32)
-        for lo, hi in HALVES:
-            for d in range(D):
-                nc.vector.tensor_tensor(
-                    terms[d][:, lo:hi],
-                    bi[:].indirect(entries(pos_sb[d], lo, hi)),
-                    stretched_mob[d][:, lo:hi],
-                    ALU.mult,
-                )
-        for lo, hi in HALVES:
-            for d in range(D):
-                before = stretched_inf if d == 0 else sums[d - 1]
-                nc.vector.tensor_tensor(sums[d][:, lo:hi], before[:, lo:hi], terms[d][:, lo:hi], ALU.add)
-            nc.vector.tensor_tensor(force[:, lo:hi], sums[D - 1][:, lo:hi], logs[:, lo:hi], ALU.mult)
+        for c in range(BLOCKS):
+            nc.vector.scalar_tensor_tensor(
+                force[:, block(c)], logs[:, block(c)], RATE / KNEE, totals[c], ALU.mult, ALU.mult
+            )
+        for lo, hi in SPANS:
             nc.scalar.activation(escape[:, lo:hi], force[:, lo:hi], ACT.Exp, scale=-1.0)
-        for lo, hi in HALVES:
-            nc.vector.tensor_tensor(spared[:, lo:hi], escape[:, lo:hi], sus_sb[:, lo:hi], ALU.mult)
-            nc.vector.tensor_tensor(result[:, lo:hi], base[:, lo:hi], spared[:, lo:hi], ALU.subtract)
+        for lo, hi in SPANS:
+            nc.vector.scalar_tensor_tensor(lost[:, lo:hi], escape[:, lo:hi], 1.0, sus_sb[:, lo:hi], ALU.subtract, ALU.mult)
+        for lo, hi in SPANS:
+            nc.vector.scalar_tensor_tensor(
+                result[:, lo:hi], lat_sb[:, lo:hi], stay[:], lost[:, lo:hi], ALU.mult, ALU.subtract
+            )
             nc.sync.dma_start(out[:, lo:hi], result[:, lo:hi])

@@ -43,15 +43,10 @@ def tile_picked_yseir_lat_p_kernel(
 
         scale_table = sb.tile([P, T], U8, align_bytes=64)
         nc.vector.memset(scale_table[:].bitcast(I32), 0)
-        warm = sb.tile([P, 1], F32)
-        nc.vector.memset(warm[:], 0.0)
-        for q in range(4):
-            nc.scalar.dma_start(
-                scale_table[32 * q : 32 * q + 4 * PASSES, :].bitcast(I32),
-                x_scales[:, 4 * q : 4 * q + 4, :].bitcast(I32),
-            )
-        warm_out = sb.tile([P, 1], F32)
-        nc.scalar.activation(warm_out[:], warm[:], ACT.Exp)
+        zero = sb.tile([P, 1], F32)
+        nc.vector.memset(zero[:], 0.0)
+        one_first = sb.tile([P, 1], F32)
+        nc.scalar.activation(one_first[:], zero[:], ACT.Exp)
 
         offs_sb = sb.tile([P, S // 16], U16)
         nc.sync.dma_start(offs_sb[:], offs)
@@ -63,6 +58,11 @@ def tile_picked_yseir_lat_p_kernel(
             nc.sync.dma_start(word_table[g][:], x_words[g].rearrange("p c r -> p (c r)").bitcast(I32))
 
         load_words(0)
+        for q in range(4):
+            nc.sync.dma_start(
+                scale_table[32 * q : 32 * q + 4 * PASSES, :].bitcast(I32),
+                x_scales[:, 4 * q : 4 * q + 4, :].bitcast(I32),
+            )
         for g in range(PASSES):
             nc.sync.dma_start(w_raw[g][:], w_rows[g])
         load_words(1)
@@ -70,17 +70,17 @@ def tile_picked_yseir_lat_p_kernel(
         nc.sync.dma_start(inf_sb[:], inf)
         mob_sb = sb.tile([P, D, S], F32)
         nc.sync.dma_start(mob_sb[:], mob.rearrange("d p j -> p d j"))
+        pos_sb = []
+        for d, pos in enumerate((pos1, pos2, pos3)):
+            lst = sb.tile([P, S // 16], U16, name=f"pos_sb{d}")
+            nc.sync.dma_start(lst[:], pos)
+            pos_sb.append(lst)
         sus_sb = sb.tile([P, S], F32)
         nc.sync.dma_start(sus_sb[:], sus)
         lat_sb = sb.tile([P, S], F32)
         nc.sync.dma_start(lat_sb[:], lat)
         rate_sb = sb.tile([P, 1], F32)
         nc.sync.dma_start(rate_sb[:], rate)
-        pos_sb = []
-        for d, pos in enumerate((pos1, pos2, pos3)):
-            lst = sb.tile([P, S // 16], U16, name=f"pos_sb{d}")
-            nc.sync.dma_start(lst[:], pos)
-            pos_sb.append(lst)
 
         ident = sb.tile([P, P], F32)
         make_identity(nc, ident[:])
@@ -144,58 +144,63 @@ def tile_picked_yseir_lat_p_kernel(
         def block(c):
             return slice(c * P, (c + 1) * P)
 
-        turned = {c: banks[2 + c][:, 0:P] for c in range(1, BLOCKS)}
-        for c in range(1, BLOCKS):
+        turned = [banks[3 + c][:, 0:P] for c in range(TURNED)]
+        for c in range(TURNED):
             nc.tensor.matmul(turned[c], lhsT=own[:, block(c)], rhs=ident[:], is_transpose=True, start=True, stop=False)
 
         logs = sb.tile([P, S], F32)
         bi = sb.tile([P, S], F32)
         for lo, hi in HALVES:
-            nc.scalar.activation(logs[:, lo:hi], capped[:, lo:hi], ACT.Ln, bias=1.0)
+            nc.scalar.activation(logs[:, lo:hi], capped[:, lo:hi], ACT.Ln, bias=one_first[:])
             nc.vector.scalar_tensor_tensor(bi[:, lo:hi], logs[:, lo:hi], RATE / KNEE, own[:, lo:hi], ALU.mult, ALU.mult)
-        warm2 = sb.tile([P, 1], F32)
-        nc.scalar.activation(warm2[:], logs[:, S - 1 : S], ACT.Exp)
+        one = sb.tile([P, 1], F32)
+        nc.scalar.activation(one[:], logs[:, S - 1 : S], ACT.Exp, scale=0.0)
 
-        escape = sb.tile([P, S], F32)
+        def neighbour_term(lo, hi, d):
+            term = sb.tile([P, hi - lo], F32, name=f"term{lo}_{d}")
+            nc.vector.tensor_tensor(term[:], bi[:].indirect(entries(pos_sb[d], lo, hi)), share[:, d, lo:hi], ALU.mult)
+            return term
 
-        def neighbour_term(dst, c, d):
-            nc.vector.tensor_tensor(
-                dst, bi[:].indirect(entries(pos_sb[d], c * P, (c + 1) * P)), share[:, d, block(c)], ALU.mult
-            )
+        def force_of(c, dst, total):
+            nc.vector.scalar_tensor_tensor(dst, logs[:, block(c)], RATE / KNEE, total, ALU.mult, ALU.mult)
 
-        totals = {}
-        for c in range(1, BLOCKS):
+        for lo, hi in SPANS[:-1]:
             for d in range(D):
-                if c == BLOCKS - 1 and d == D - 1:
-                    term = escape[:, S // 2 - P // 2 : S // 2 + P // 2]
-                else:
-                    term = sb.tile([P, P], F32, name=f"term{c}_{d}")[:]
-                neighbour_term(term, c, d)
-                nc.tensor.matmul(turned[c], lhsT=term, rhs=ident[:], is_transpose=True, start=False, stop=(d == D - 1))
+                term = neighbour_term(lo, hi, d)
+                for c in range(lo // P, hi // P):
+                    nc.tensor.matmul(
+                        turned[c],
+                        lhsT=term[:, c * P - lo : (c + 1) * P - lo],
+                        rhs=ident[:],
+                        is_transpose=True,
+                        start=False,
+                        stop=(d == D - 1),
+                    )
+        direct = [neighbour_term(TURNED * P, S, d) for d in range(D)]
+        running = sb.tile([P, P], F32)
+        nc.vector.tensor_tensor(running[:], own[:, block(TURNED)], direct[0][:], ALU.add)
+        force = sb.tile([P, TURNED * P], F32)
+        for c in range(TURNED):
             turned_sb = sb.tile([P, P], F32, name=f"turned_sb{c}")
             nc.scalar.copy(turned_sb[:], turned[c])
-            totals[c] = banks[(5 + c) % 8][:, 0:P]
-            nc.tensor.transpose(totals[c], turned_sb[:], ident[:])
-        running = own[:, block(0)]
-        for d in range(D):
-            term = sb.tile([P, P], F32, name=f"term0_{d}")
-            neighbour_term(term[:], 0, d)
-            summed = sb.tile([P, P], F32, name=f"summed{d}")
-            nc.vector.tensor_tensor(summed[:], running, term[:], ALU.add)
-            running = summed[:]
-        totals[0] = running
+            total = banks[(6 + c) % 8][:, 0:P]
+            nc.tensor.transpose(total, turned_sb[:], ident[:])
+            force_of(c, force[:, block(c)], total)
+            if c + 1 < D:
+                nc.vector.tensor_tensor(turned_sb[:], running[:], direct[c + 1][:], ALU.add)
+            else:
+                force_of(TURNED, turned_sb[:], running[:])
+            running = turned_sb
 
-        force = sb.tile([P, S], F32)
+        escape = sb.tile([P, S], F32)
         lost = sb.tile([P, S], F32)
         result = sb.tile([P, S], F32)
-        for c in range(BLOCKS):
+        for lo, hi in SPANS:
+            nc.scalar.activation(escape[:, lo:hi], force[:, lo:hi] if hi < S else running[:], ACT.Exp, scale=-1.0)
+        for lo, hi in SPANS:
             nc.vector.scalar_tensor_tensor(
-                force[:, block(c)], logs[:, block(c)], RATE / KNEE, totals[c], ALU.mult, ALU.mult
+                lost[:, lo:hi], escape[:, lo:hi], one[:], sus_sb[:, lo:hi], ALU.subtract, ALU.mult
             )
-        for lo, hi in SPANS:
-            nc.scalar.activation(escape[:, lo:hi], force[:, lo:hi], ACT.Exp, scale=-1.0)
-        for lo, hi in SPANS:
-            nc.vector.scalar_tensor_tensor(lost[:, lo:hi], escape[:, lo:hi], 1.0, sus_sb[:, lo:hi], ALU.subtract, ALU.mult)
         for lo, hi in SPANS:
             nc.vector.scalar_tensor_tensor(
                 result[:, lo:hi], lat_sb[:, lo:hi], stay[:], lost[:, lo:hi], ALU.mult, ALU.subtract

@@ -20,16 +20,28 @@ ACT = mybir.ActivationFunctionType
 P = 128
 PACK = 4
 PASSES = K // (P * PACK)
-BLOCKS = S // P
-TURNED = BLOCKS - 1
-HALVES = [(0, 256), (256, 512)]
-KNEE = 32.0
+QUADRANT = 32
+SCALE_ROWS = 4
+LIST_ROWS = 16
+BANKS = 8
+TURNED = S // P - 1
 RATE = 0.6
-SPANS = [(0, 256), (256, 384), (384, 512)]
+KNEE = 32.0
+SLOPE = -RATE / KNEE
+
+HALVES = [(0, S // 2), (S // 2, S)]
+SPANS = [(0, 2 * P), (2 * P, 3 * P), (3 * P, S)]
+
+assert TURNED == D
+assert len(SPANS) + TURNED + TURNED - 1 == BANKS
 
 
 def entries(lst, lo, hi):
-    return lst[:, lo // 16 : hi // 16]
+    return lst[:, lo // LIST_ROWS : hi // LIST_ROWS]
+
+
+def block(c):
+    return slice(c * P, (c + 1) * P)
 
 
 def tile_picked_yseir_lat_p_kernel(
@@ -39,29 +51,32 @@ def tile_picked_yseir_lat_p_kernel(
     with ExitStack() as ctx:
         sb = ctx.enter_context(tc.tile_pool(name="sb", bufs=1))
         ps = ctx.enter_context(tc.psum_pool(name="ps", bufs=1))
-        banks = [ps.tile([P, S], F32, name=f"bank{b}") for b in range(8)]
+        banks = [ps.tile([P, S], F32, name=f"bank{b}") for b in range(BANKS)]
+        y = [banks[n][:, 0 : hi - lo] for n, (lo, hi) in enumerate(SPANS)]
+        turned = [banks[len(SPANS) + c][:, 0:P] for c in range(TURNED)]
+        totals = [banks[(len(SPANS) + TURNED + c) % BANKS][:, 0:P] for c in range(TURNED)]
 
         scale_table = sb.tile([P, T], U8, align_bytes=64)
         nc.vector.memset(scale_table[:].bitcast(I32), 0)
         zero = sb.tile([P, 1], F32)
         nc.vector.memset(zero[:], 0.0)
-        one_first = sb.tile([P, 1], F32)
-        nc.scalar.activation(one_first[:], zero[:], ACT.Exp)
+        half = sb.tile([P, 1], F32)
+        nc.scalar.activation(half[:], zero[:], ACT.Sigmoid)
 
-        offs_sb = sb.tile([P, S // 16], U16)
+        offs_sb = sb.tile([P, S // LIST_ROWS], U16)
         nc.sync.dma_start(offs_sb[:], offs)
         word_table = [sb.tile([P, T], I32, name=f"word_table{g}", align_bytes=64) for g in range(PASSES)]
         w_raw = [sb.tile([P, PACK, M], F32, name=f"w_raw{g}") for g in range(PASSES)]
-        w_rows = w1.rearrange("(g p j) m -> g p j m", g=PASSES, j=PACK)
+        w_rows = w1.rearrange("(g p t) m -> g p t m", g=PASSES, t=PACK)
 
         def load_words(g):
-            nc.sync.dma_start(word_table[g][:], x_words[g].rearrange("p c r -> p (c r)").bitcast(I32))
+            nc.sync.dma_start(word_table[g][:], x_words[g].rearrange("p c t -> p (c t)").bitcast(I32))
 
         load_words(0)
-        for q in range(4):
+        for q in range(P // QUADRANT):
             nc.sync.dma_start(
-                scale_table[32 * q : 32 * q + 4 * PASSES, :].bitcast(I32),
-                x_scales[:, 4 * q : 4 * q + 4, :].bitcast(I32),
+                scale_table[QUADRANT * q : QUADRANT * q + SCALE_ROWS * PASSES, :].bitcast(I32),
+                x_scales[:, SCALE_ROWS * q : SCALE_ROWS * (q + 1), :].bitcast(I32),
             )
         for g in range(PASSES):
             nc.sync.dma_start(w_raw[g][:], w_rows[g])
@@ -72,7 +87,7 @@ def tile_picked_yseir_lat_p_kernel(
         nc.sync.dma_start(mob_sb[:], mob.rearrange("d p j -> p d j"))
         pos_sb = []
         for d, pos in enumerate((pos1, pos2, pos3)):
-            lst = sb.tile([P, S // 16], U16, name=f"pos_sb{d}")
+            lst = sb.tile([P, S // LIST_ROWS], U16, name=f"pos_sb{d}")
             nc.sync.dma_start(lst[:], pos)
             pos_sb.append(lst)
         sus_sb = sb.tile([P, S], F32)
@@ -89,50 +104,48 @@ def tile_picked_yseir_lat_p_kernel(
         w_codes = sb.tile([P, PASSES * M], U32, align_bytes=64)
         w_scales = sb.tile([P, PASSES * M], U8, align_bytes=64)
         x_codes = [sb.tile([P, S], U32, name=f"x_codes{g}", align_bytes=64) for g in range(PASSES)]
-        x_sc = sb.tile([P, S], U8, align_bytes=64)
+        x_picked_scales = sb.tile([P, S], U8, align_bytes=64)
 
         def product(g, n):
             lo, hi = SPANS[n]
             nc.tensor.matmul_mx(
-                out=banks[n][:, 0 : hi - lo],
+                out=y[n],
                 lhsT=w_codes[:, g * M : (g + 1) * M].bitcast(FP8X4),
                 lhsT_scale=w_scales[:, g * M : (g + 1) * M],
                 rhs=x_codes[g][:, lo:hi].bitcast(FP8X4),
-                rhs_scale=x_sc[4 * g :, lo:hi],
+                rhs_scale=x_picked_scales[SCALE_ROWS * g :, lo:hi],
                 start=(g == 0),
                 stop=(g == PASSES - 1),
             )
 
         nc.vector.tensor_copy(x_codes[0][:], word_table[0][:].bitcast(U32).indirect(offs_sb[:]))
-        nc.vector.tensor_copy(x_sc[:], scale_table[:].indirect(offs_sb[:]))
+        nc.vector.tensor_copy(x_picked_scales[:], scale_table[:].indirect(offs_sb[:]))
         for g in range(PASSES):
             nc.scalar.copy(
-                w_bf[:, g * M * PACK : (g + 1) * M * PACK].rearrange("p (c i j) -> p c j i", i=4, j=PACK),
-                w_raw[g][:].rearrange("p j (c i) -> p c j i", i=4),
+                w_bf[:, g * M * PACK : (g + 1) * M * PACK].rearrange("p (c i t) -> p c t i", i=4, t=PACK),
+                w_raw[g][:].rearrange("p t (c i) -> p c t i", i=4),
             )
         nc.vector.quantize_mx(out=w_codes[:].bitcast(FP8X4), scales=w_scales[:], in_=w_bf[:])
         for n in range(len(SPANS)):
             product(0, n)
-        growth = sb.tile([P, S], F32)
+        sig = sb.tile([P, S], F32)
         for n, (lo, hi) in enumerate(SPANS):
             nc.vector.tensor_copy(
                 x_codes[1][:, lo:hi], word_table[1][:].bitcast(U32).indirect(entries(offs_sb, lo, hi))
             )
             product(1, n)
-            nc.scalar.activation(growth[:, lo:hi], banks[n][:, 0 : hi - lo], ACT.Exp)
+            nc.scalar.activation(sig[:, lo:hi], y[n], ACT.Sigmoid, scale=-1.0)
 
-        capped = sb.tile([P, S], F32)
-        nc.vector.tensor_scalar(capped[:], growth[:], math.exp(KNEE), None, ALU.min)
+        floored_half = sb.tile([P, S], F32)
+        nc.vector.tensor_scalar(floored_half[:], sig[:], math.exp(-KNEE), half[:], ALU.max, ALU.mult)
         own = sb.tile([P, S], F32)
         for n, (lo, hi) in enumerate(SPANS):
-            nc.vector.scalar_tensor_tensor(
-                own[:, lo:hi], banks[n][:, 0 : hi - lo], KNEE, inf_sb[:, lo:hi], ALU.max, ALU.mult
-            )
+            nc.vector.scalar_tensor_tensor(own[:, lo:hi], y[n], KNEE, inf_sb[:, lo:hi], ALU.max, ALU.mult)
         share = sb.tile([P, D, S], F32)
         for n, (lo, hi) in enumerate(SPANS):
             nc.vector.scalar_tensor_tensor(
                 share[:, :, lo:hi],
-                banks[n][:, 0 : hi - lo].unsqueeze(1).to_broadcast([P, D, hi - lo]),
+                y[n].unsqueeze(1).to_broadcast([P, D, hi - lo]),
                 KNEE,
                 mob_sb[:, :, lo:hi],
                 ALU.max,
@@ -141,18 +154,14 @@ def tile_picked_yseir_lat_p_kernel(
         stay = sb.tile([P, 1], F32)
         nc.vector.tensor_scalar(stay[:], rate_sb[:], -1.0, 1.0, ALU.mult, ALU.add)
 
-        def block(c):
-            return slice(c * P, (c + 1) * P)
-
-        turned = [banks[3 + c][:, 0:P] for c in range(TURNED)]
         for c in range(TURNED):
             nc.tensor.matmul(turned[c], lhsT=own[:, block(c)], rhs=ident[:], is_transpose=True, start=True, stop=False)
 
         logs = sb.tile([P, S], F32)
         bi = sb.tile([P, S], F32)
         for lo, hi in HALVES:
-            nc.scalar.activation(logs[:, lo:hi], capped[:, lo:hi], ACT.Ln, bias=one_first[:])
-            nc.vector.scalar_tensor_tensor(bi[:, lo:hi], logs[:, lo:hi], RATE / KNEE, own[:, lo:hi], ALU.mult, ALU.mult)
+            nc.scalar.activation(logs[:, lo:hi], floored_half[:, lo:hi], ACT.Ln, scale=2.0)
+            nc.vector.scalar_tensor_tensor(bi[:, lo:hi], logs[:, lo:hi], SLOPE, own[:, lo:hi], ALU.mult, ALU.mult)
         one = sb.tile([P, 1], F32)
         nc.scalar.activation(one[:], logs[:, S - 1 : S], ACT.Exp, scale=0.0)
 
@@ -162,7 +171,7 @@ def tile_picked_yseir_lat_p_kernel(
             return term
 
         def force_of(c, dst, total):
-            nc.vector.scalar_tensor_tensor(dst, logs[:, block(c)], RATE / KNEE, total, ALU.mult, ALU.mult)
+            nc.vector.scalar_tensor_tensor(dst, logs[:, block(c)], SLOPE, total, ALU.mult, ALU.mult)
 
         for lo, hi in SPANS[:-1]:
             for d in range(D):
@@ -176,27 +185,26 @@ def tile_picked_yseir_lat_p_kernel(
                         start=False,
                         stop=(d == D - 1),
                     )
-        direct = [neighbour_term(TURNED * P, S, d) for d in range(D)]
-        running = sb.tile([P, P], F32)
-        nc.vector.tensor_tensor(running[:], own[:, block(TURNED)], direct[0][:], ALU.add)
+        last_terms = [neighbour_term(TURNED * P, S, d) for d in range(D)]
+        last = sb.tile([P, P], F32)
+        nc.vector.tensor_tensor(last[:], own[:, block(TURNED)], last_terms[0][:], ALU.add)
         force = sb.tile([P, TURNED * P], F32)
         for c in range(TURNED):
-            turned_sb = sb.tile([P, P], F32, name=f"turned_sb{c}")
-            nc.scalar.copy(turned_sb[:], turned[c])
-            total = banks[(6 + c) % 8][:, 0:P]
-            nc.tensor.transpose(total, turned_sb[:], ident[:])
-            force_of(c, force[:, block(c)], total)
+            staging = sb.tile([P, P], F32, name=f"staging{c}")
+            nc.scalar.copy(staging[:], turned[c])
+            nc.tensor.transpose(totals[c], staging[:], ident[:])
+            force_of(c, force[:, block(c)], totals[c])
             if c + 1 < D:
-                nc.vector.tensor_tensor(turned_sb[:], running[:], direct[c + 1][:], ALU.add)
+                nc.vector.tensor_tensor(staging[:], last[:], last_terms[c + 1][:], ALU.add)
             else:
-                force_of(TURNED, turned_sb[:], running[:])
-            running = turned_sb
+                force_of(TURNED, staging[:], last[:])
+            last = staging
 
         escape = sb.tile([P, S], F32)
         lost = sb.tile([P, S], F32)
         result = sb.tile([P, S], F32)
         for lo, hi in SPANS:
-            nc.scalar.activation(escape[:, lo:hi], force[:, lo:hi] if hi < S else running[:], ACT.Exp, scale=-1.0)
+            nc.scalar.activation(escape[:, lo:hi], force[:, lo:hi] if hi < S else last[:], ACT.Exp, scale=-1.0)
         for lo, hi in SPANS:
             nc.vector.scalar_tensor_tensor(
                 lost[:, lo:hi], escape[:, lo:hi], one[:], sus_sb[:, lo:hi], ALU.subtract, ALU.mult

import math
from contextlib import ExitStack

import concourse.mybir as mybir
from concourse.masks import make_identity

K, T, S, M, D = 1024, 1024, 512, 128, 3
FLOPS = 2 * K * M * S

F32 = mybir.dt.float32
BF16 = mybir.dt.bfloat16
I32 = mybir.dt.int32
U32 = mybir.dt.uint32
U16 = mybir.dt.uint16
U8 = mybir.dt.uint8
FP8X4 = mybir.dt.float8_e4m3fn_x4
ALU = mybir.AluOpType
ACT = mybir.ActivationFunctionType

P = 128
PACK = 4
PASSES = K // (P * PACK)
QUADRANT = 32
SCALE_ROWS = 4
LIST_ROWS = 16
BANKS = 8
TURNED = S // P - 1
RATE = 0.6
KNEE = 32.0
SLOPE = -RATE / KNEE

HALVES = [(0, S // 2), (S // 2, S)]
SPANS = [(0, 2 * P), (2 * P, 3 * P), (3 * P, S)]

assert TURNED == D
assert len(SPANS) + TURNED + TURNED - 1 == BANKS


def entries(lst, lo, hi):
    return lst[:, lo // LIST_ROWS : hi // LIST_ROWS]


def block(c):
    return slice(c * P, (c + 1) * P)


def tile_picked_yseir_lat_p_kernel(
    tc, x_words, x_scales, w1, sus, inf, lat, mob, rate, offs, pos1, pos2, pos3, out
):
    nc = tc.nc
    with ExitStack() as ctx:
        sb = ctx.enter_context(tc.tile_pool(name="sb", bufs=1))
        ps = ctx.enter_context(tc.psum_pool(name="ps", bufs=1))
        banks = [ps.tile([P, S], F32, name=f"bank{b}") for b in range(BANKS)]
        y = [banks[n][:, 0 : hi - lo] for n, (lo, hi) in enumerate(SPANS)]
        turned = [banks[len(SPANS) + c][:, 0:P] for c in range(TURNED)]
        totals = [banks[(len(SPANS) + TURNED + c) % BANKS][:, 0:P] for c in range(TURNED)]

        scale_table = sb.tile([P, T], U8, align_bytes=64)
        nc.vector.memset(scale_table[:].bitcast(I32), 0)
        zero = sb.tile([P, 1], F32)
        nc.vector.memset(zero[:], 0.0)
        half = sb.tile([P, 1], F32)
        nc.scalar.activation(half[:], zero[:], ACT.Sigmoid)

        offs_sb = sb.tile([P, S // LIST_ROWS], U16)
        nc.sync.dma_start(offs_sb[:], offs)
        word_table = [sb.tile([P, T], I32, name=f"word_table{g}", align_bytes=64) for g in range(PASSES)]
        w_raw = [sb.tile([P, PACK, M], F32, name=f"w_raw{g}") for g in range(PASSES)]
        w_rows = w1.rearrange("(g p t) m -> g p t m", g=PASSES, t=PACK)

        def load_words(g):
            nc.sync.dma_start(word_table[g][:], x_words[g].rearrange("p c t -> p (c t)").bitcast(I32))

        load_words(0)
        for q in range(P // QUADRANT):
            nc.sync.dma_start(
                scale_table[QUADRANT * q : QUADRANT * q + SCALE_ROWS * PASSES, :].bitcast(I32),
                x_scales[:, SCALE_ROWS * q : SCALE_ROWS * (q + 1), :].bitcast(I32),
            )
        for g in range(PASSES):
            nc.sync.dma_start(w_raw[g][:], w_rows[g])
        load_words(1)
        inf_sb = sb.tile([P, S], F32)
        nc.sync.dma_start(inf_sb[:], inf)
        mob_sb = sb.tile([P, D, S], F32)
        nc.sync.dma_start(mob_sb[:], mob.rearrange("d p j -> p d j"))
        pos_sb = []
        for d, pos in enumerate((pos1, pos2, pos3)):
            lst = sb.tile([P, S // LIST_ROWS], U16, name=f"pos_sb{d}")
            nc.sync.dma_start(lst[:], pos)
            pos_sb.append(lst)
        sus_sb = sb.tile([P, S], F32)
        nc.sync.dma_start(sus_sb[:], sus)
        lat_sb = sb.tile([P, S], F32)
        nc.sync.dma_start(lat_sb[:], lat)
        rate_sb = sb.tile([P, 1], F32)
        nc.sync.dma_start(rate_sb[:], rate)

        ident = sb.tile([P, P], F32)
        make_identity(nc, ident[:])

        w_bf = sb.tile([P, PASSES * M * PACK], BF16, align_bytes=64)
        w_codes = sb.tile([P, PASSES * M], U32, align_bytes=64)
        w_scales = sb.tile([P, PASSES * M], U8, align_bytes=64)
        x_codes = [sb.tile([P, S], U32, name=f"x_codes{g}", align_bytes=64) for g in range(PASSES)]
        x_picked_scales = sb.tile([P, S], U8, align_bytes=64)

        def product(g, n):
            lo, hi = SPANS[n]
            nc.tensor.matmul_mx(
                out=y[n],
                lhsT=w_codes[:, g * M : (g + 1) * M].bitcast(FP8X4),
                lhsT_scale=w_scales[:, g * M : (g + 1) * M],
                rhs=x_codes[g][:, lo:hi].bitcast(FP8X4),
                rhs_scale=x_picked_scales[SCALE_ROWS * g :, lo:hi],
                start=(g == 0),
                stop=(g == PASSES - 1),
            )

        nc.vector.tensor_copy(x_codes[0][:], word_table[0][:].bitcast(U32).indirect(offs_sb[:]))
        nc.vector.tensor_copy(x_picked_scales[:], scale_table[:].indirect(offs_sb[:]))
        for g in range(PASSES):
            nc.scalar.copy(
                w_bf[:, g * M * PACK : (g + 1) * M * PACK].rearrange("p (c i t) -> p c t i", i=4, t=PACK),
                w_raw[g][:].rearrange("p t (c i) -> p c t i", i=4),
            )
        nc.vector.quantize_mx(out=w_codes[:].bitcast(FP8X4), scales=w_scales[:], in_=w_bf[:])
        for n in range(len(SPANS)):
            product(0, n)
        sig = sb.tile([P, S], F32)
        for n, (lo, hi) in enumerate(SPANS):
            nc.vector.tensor_copy(
                x_codes[1][:, lo:hi], word_table[1][:].bitcast(U32).indirect(entries(offs_sb, lo, hi))
            )
            product(1, n)
            nc.scalar.activation(sig[:, lo:hi], y[n], ACT.Sigmoid, scale=-1.0)

        floored_half = sb.tile([P, S], F32)
        nc.vector.tensor_scalar(floored_half[:], sig[:], math.exp(-KNEE), half[:], ALU.max, ALU.mult)
        own = sb.tile([P, S], F32)
        for n, (lo, hi) in enumerate(SPANS):
            nc.vector.scalar_tensor_tensor(own[:, lo:hi], y[n], KNEE, inf_sb[:, lo:hi], ALU.max, ALU.mult)
        share = sb.tile([P, D, S], F32)
        for n, (lo, hi) in enumerate(SPANS):
            nc.vector.scalar_tensor_tensor(
                share[:, :, lo:hi],
                y[n].unsqueeze(1).to_broadcast([P, D, hi - lo]),
                KNEE,
                mob_sb[:, :, lo:hi],
                ALU.max,
                ALU.mult,
            )
        stay = sb.tile([P, 1], F32)
        nc.vector.tensor_scalar(stay[:], rate_sb[:], -1.0, 1.0, ALU.mult, ALU.add)

        for c in range(TURNED):
            nc.tensor.matmul(turned[c], lhsT=own[:, block(c)], rhs=ident[:], is_transpose=True, start=True, stop=False)

        logs = sb.tile([P, S], F32)
        bi = sb.tile([P, S], F32)
        for lo, hi in HALVES:
            nc.scalar.activation(logs[:, lo:hi], floored_half[:, lo:hi], ACT.Ln, scale=2.0)
            nc.vector.scalar_tensor_tensor(bi[:, lo:hi], logs[:, lo:hi], SLOPE, own[:, lo:hi], ALU.mult, ALU.mult)
        one = sb.tile([P, 1], F32)
        nc.scalar.activation(one[:], logs[:, S - 1 : S], ACT.Exp, scale=0.0)

        def neighbour_term(lo, hi, d):
            term = sb.tile([P, hi - lo], F32, name=f"term{lo}_{d}")
            nc.vector.tensor_tensor(term[:], bi[:].indirect(entries(pos_sb[d], lo, hi)), share[:, d, lo:hi], ALU.mult)
            return term

        def force_of(c, dst, total):
            nc.vector.scalar_tensor_tensor(dst, logs[:, block(c)], SLOPE, total, ALU.mult, ALU.mult)

        for lo, hi in SPANS[:-1]:
            for d in range(D):
                term = neighbour_term(lo, hi, d)
                for c in range(lo // P, hi // P):
                    nc.tensor.matmul(
                        turned[c],
                        lhsT=term[:, c * P - lo : (c + 1) * P - lo],
                        rhs=ident[:],
                        is_transpose=True,
                        start=False,
                        stop=(d == D - 1),
                    )
        last_terms = [neighbour_term(TURNED * P, S, d) for d in range(D)]
        last = sb.tile([P, P], F32)
        nc.vector.tensor_tensor(last[:], own[:, block(TURNED)], last_terms[0][:], ALU.add)
        force = sb.tile([P, TURNED * P], F32)
        for c in range(TURNED):
            staging = sb.tile([P, P], F32, name=f"staging{c}")
            nc.scalar.copy(staging[:], turned[c])
            nc.tensor.transpose(totals[c], staging[:], ident[:])
            force_of(c, force[:, block(c)], totals[c])
            if c + 1 < D:
                nc.vector.tensor_tensor(staging[:], last[:], last_terms[c + 1][:], ALU.add)
            else:
                force_of(TURNED, staging[:], last[:])
            last = staging

        escape = sb.tile([P, S], F32)
        lost = sb.tile([P, S], F32)
        result = sb.tile([P, S], F32)
        for lo, hi in SPANS:
            nc.scalar.activation(escape[:, lo:hi], force[:, lo:hi] if hi < S else last[:], ACT.Exp, scale=-1.0)
        for lo, hi in SPANS:
            nc.vector.scalar_tensor_tensor(
                lost[:, lo:hi], escape[:, lo:hi], one[:], sus_sb[:, lo:hi], ALU.subtract, ALU.mult
            )
        for lo, hi in SPANS:
            nc.vector.scalar_tensor_tensor(
                result[:, lo:hi], lat_sb[:, lo:hi], stay[:], lost[:, lo:hi], ALU.mult, ALU.subtract
            )
            nc.sync.dma_start(out[:, lo:hi], result[:, lo:hi])
